import numpy as np
import ml_dtypes


def mxq(x, axis, fmt="e4m3"):
    dtype, down = {"e4m3": (ml_dtypes.float8_e4m3fn, 7), "e5m2": (ml_dtypes.float8_e5m2, 14)}[fmt]
    v = np.moveaxis(np.asarray(x, np.float32).astype(ml_dtypes.bfloat16).astype(np.float64), axis, -1)
    blocks = v.reshape(v.shape[:-1] + (-1, 32))
    amax = np.abs(blocks).max(-1, keepdims=True)
    byte = np.maximum(np.where(amax > 0, np.frexp(amax)[1] - 1 + 127, 0) - down, 1)
    scale = np.exp2(byte - 127.0)
    codes = (blocks / scale).astype(np.float32).astype(dtype).astype(np.float64)
    return np.moveaxis((codes * scale).reshape(v.shape), -1, axis)


WIDE = False


def mx_kscale(k):
    if not WIDE:
        return np.ones(k)
    levels = np.array([10, -10, 5, -5, 0])
    if k % 512:
        return np.exp2(np.random.permutation(np.resize(levels, k // 32))).repeat(32)
    a = np.empty((k // 512, 16))
    for p in range(k // 512):
        a[p, :8] = np.random.permutation(np.resize(levels, 8))
        for g in range(8):
            far = levels[np.abs(levels - a[p, g]) >= 10]
            a[p, g + 8] = far[np.random.randint(len(far))]
    return np.exp2(a.ravel()).repeat(32)


def f64(x):
    return np.asarray(x).astype(np.float64)


def striped(idx):
    return np.tile(idx.reshape(-1, 16).T, (8, 1)).astype(np.uint16)


def unstriped(offs):
    return offs[:16].T.reshape(-1).astype(np.int64)


def striped8(idx):
    return np.concatenate([x.reshape(-1, 16).T for x in idx]).astype(np.uint16)


def runs(offs, k):
    lists = np.stack([offs[16 * r : 16 * r + 16].T.reshape(-1) for r in range(8)]).astype(np.int64)
    return lists[np.arange(k) % 512 // 64]


def pack_weight(w):
    k, n = w.shape
    w = f64(np.asarray(w, np.float32).astype(ml_dtypes.bfloat16)).reshape(k // 32, 32, n)
    amax = np.abs(w).max(1)
    byte = np.clip(np.where(amax > 0, np.frexp(amax)[1] - 1 + 127 - 7, 1), 1, 254)
    scaled = (w * np.exp2(127.0 - byte)[:, None, :]).reshape(k, n).astype(np.float32)
    words = np.ascontiguousarray(scaled.reshape(k // 512, 128, 4, n).transpose(0, 1, 3, 2)).astype(ml_dtypes.float8_e4m3fn).view(np.uint8)
    return words, np.ascontiguousarray(byte.astype(np.uint8).reshape(k // 512, 16, n))


def unpack_weight(words, scales):
    g, p, n, _ = words.shape
    vals = np.ascontiguousarray(words).view(ml_dtypes.float8_e4m3fn).astype(np.float64) * np.repeat(np.exp2(scales.astype(np.float64) - 127.0), 8, axis=1)[..., None]
    return vals.transpose(0, 1, 3, 2).reshape(g * 512, n)


E2M1 = np.array([0.0, 0.5, 1.0, 1.5, 2.0, 3.0, 4.0, 6.0, -0.0, -0.5, -1.0, -1.5, -2.0, -3.0, -4.0, -6.0])


def pack_fp4(w):
    k, n = w.shape
    w = f64(np.asarray(w, np.float32).astype(ml_dtypes.bfloat16)).reshape(k // 32, 32, n)
    amax = np.abs(w).max(1)
    mant, ex = np.frexp(amax / 6.0)
    byte = np.clip(np.where(amax > 0, np.where(mant > 0.5, ex, ex - 1) + 127, 1), 1, 254)
    scaled = (w * np.exp2(127.0 - byte)[:, None, :]).reshape(k, n).astype(np.float32)
    c = np.ascontiguousarray(scaled.reshape(k // 512, 128, 4, n).transpose(0, 1, 3, 2)).astype(ml_dtypes.float4_e2m1fn).view(np.uint8) & 0xF
    words = (c[..., 0::2] | (c[..., 1::2] << 4)).reshape(k // 512, 128, 2 * n)
    return np.ascontiguousarray(words), np.ascontiguousarray(byte.astype(np.uint8).reshape(k // 512, 16, n))


def unpack_fp4(words, scales):
    g, _, n = scales.shape
    words = np.ascontiguousarray(words).reshape(g, 128, n, 2)
    nib = np.empty((g, 128, n, 4), np.uint8)
    nib[..., 0::2] = words & 0xF
    nib[..., 1::2] = words >> 4
    vals = E2M1[nib] * np.repeat(np.exp2(scales.astype(np.float64) - 127.0), 8, axis=1)[..., None]
    return vals.transpose(0, 1, 3, 2).reshape(g * 512, n)


def sigmoid(v):
    return 1.0 / (1.0 + np.exp(-np.maximum(v, -700.0)))

def planes(y):
    n, m = y.shape
    v = y.astype(np.float32).astype(ml_dtypes.bfloat16).astype(np.float64).reshape(n // 32, 32, m)
    top = np.abs(v).max(1)
    byte = np.clip(np.where(top > 0, np.frexp(top)[1] - 1 + 127 - 7, 1), 1, 254)
    codes = (v * np.exp2(127.0 - byte)[:, None, :]).reshape(n, m).astype(np.float32).astype(ml_dtypes.float8_e4m3fn).view(np.uint8)
    words = codes.reshape(n // 512, 128, 4, m).transpose(0, 1, 3, 2)
    return np.ascontiguousarray(words), np.ascontiguousarray(byte.astype(np.uint8).reshape(n // 512, 16, m))


K, T, S, H, G = 512, 2048, 256, 512, 2048


def setup_inputs():
    n = np.random.standard_normal
    s = mx_kscale(K)[:, None]
    packed_xT = pack_weight(n((K, T)) * s)
    packed_w1 = pack_fp4(n((K, H)) / np.sqrt(K) / s)
    packed_dT = pack_weight(n((K, G)) / s)
    return {
        "x_words": packed_xT[0],
        "x_scales": packed_xT[1],
        "w1_words": packed_w1[0],
        "w1_scales": packed_w1[1],
        "tau": np.random.uniform(0.2, 0.6, (H, 1)).astype(np.float32),
        "tau2": np.random.uniform(0.6, 1.0, (H, 1)).astype(np.float32),
        "gs": (np.random.uniform(0.5, 1.5, (K, 1)) * s).astype(np.float32),
        "d_words": packed_dT[0],
        "d_scales": packed_dT[1],
        "sl": np.random.uniform(1.5, 2.5, (H, 1)).astype(np.float32),
        "lo": np.random.uniform(-1.2, -0.4, (H, 1)).astype(np.float32),
        "hi": np.random.uniform(0.4, 1.2, (H, 1)).astype(np.float32),
        "offs": striped(np.random.permutation(T)[:S]),
        "n1": striped(np.random.permutation(S)),
        "n2": striped(np.random.permutation(S)),
        "k1": striped8(np.random.randint(0, G, (8, H))),
        "n3": striped8(np.stack([np.random.permutation(S) for _ in range(8)])),
    }


def reference(x_words, x_scales, w1_words, w1_scales, tau, tau2, gs, d_words, d_scales, sl, lo, hi, offs, n1, n2, k1, n3):
    d_k1 = unpack_weight(d_words, d_scales)[np.arange(K)[:, None], runs(k1, K)]
    xq = unpack_weight(x_words, x_scales)[:, unstriped(offs)]
    y = unpack_fp4(w1_words, w1_scales).T @ xq
    top = y.max(axis=1, keepdims=True)
    ea = np.exp(f64(tau) * (y[:, unstriped(n1)] - top))
    ea2 = np.exp(f64(tau2) * (y[:, unstriped(n2)] - top))
    z = f64(gs) * (3.0 * (ea - ea2))
    h = 0.0625 * ((d_k1.T @ mxq(z, 0, "e4m3")))
    sg = sigmoid(f64(sl) * (h[np.arange(H)[:, None], runs(n3, H)] - f64(lo)))
    sg2 = sigmoid(f64(sl) * (h[np.arange(H)[:, None], runs(n3, H)] - f64(hi)))
    out_0 = h * (sg - sg2)
    return (out_0,) + planes(out_0)

@@ -1,0 +1,234 @@
+from contextlib import ExitStack
+
+import concourse.mybir as mybir
+
+K, T, S, H, G = 512, 2048, 256, 512, 2048
+FLOPS = 2 * K * H * S + 2 * H * H * S
+
+F32 = mybir.dt.float32
+BF16 = mybir.dt.bfloat16
+I32 = mybir.dt.int32
+U32 = mybir.dt.uint32
+U16 = mybir.dt.uint16
+U8 = mybir.dt.uint8
+FP8X4 = mybir.dt.float8_e4m3fn_x4
+FP4X4 = mybir.dt.float4_e2m1fn_x4
+ALU = mybir.AluOpType
+ACT = mybir.ActivationFunctionType
+
+P = 128
+PACK = 4
+HALF = S // 2
+LIST = 16
+
+
+def tile_picked_denseetwebd_none_po_kernel(
+    tc, x_words, x_scales, w1_words, w1_scales, tau, tau2, gs, d_words, d_scales, sl, lo, hi,
+    offs, n1, n2, k1, n3, out_0, out_1, out_2,
+):
+    nc = tc.nc
+    with ExitStack() as ctx:
+        lists = ctx.enter_context(tc.tile_pool(name="lists", bufs=1))
+        sb = ctx.enter_context(tc.tile_pool(name="sb", bufs=1))
+        psum = ctx.enter_context(tc.psum_pool(name="psum", bufs=1))
+
+        def tile(name, shape, dtype, tag=None):
+            return sb.tile(shape, dtype, name=name, tag=tag or name, align_bytes=64)
+
+        def load_list(name, src, entries):
+            held = lists.tile([P, entries // LIST], U16, name=name)
+            nc.sync.dma_start(held[:], src)
+            return held
+
+        def load_rows(name, src, queue):
+            held = tile(name, [P, PACK], F32)
+            queue.dma_start(held[:], src.rearrange("(p t) o -> p (t o)", t=PACK))
+            return held
+
+        def entries(held, first, count):
+            return held[:, first // LIST : (first + count) // LIST]
+
+        w1_scale_raw = tile("w1_scale_raw", [P, H], U8)
+        x_scale_table = tile("x_scale_table", [P, T], U8)
+        d_scale_table = tile("d_scale_table", [P, G], U8)
+        for cleared in (x_scale_table, w1_scale_raw, d_scale_table):
+            nc.vector.memset(cleared[:].bitcast(I32), 0)
+
+        offs_sb = load_list("offs_sb", offs, S)
+        tau_sb = load_rows("tau_sb", tau, nc.scalar)
+        tau2_sb = load_rows("tau2_sb", tau2, nc.scalar)
+        w1_raw = tile("w1_raw", [P, 2 * H], U8)
+        nc.gpsimd.dma_start(w1_raw[:].bitcast(I32), w1_words[0].bitcast(I32))
+        for q in range(4):
+            nc.sync.dma_start(x_scale_table[32 * q : 32 * q + 4, :].bitcast(I32), x_scales[0, 4 * q : 4 * q + 4, :].bitcast(I32))
+        x_table = tile("x_table", [P, T], I32)
+        nc.scalar.dma_start(x_table[:], x_words[0].rearrange("p c r -> p (c r)").bitcast(I32))
+        for q in range(4):
+            nc.sync.dma_start(w1_scale_raw[32 * q : 32 * q + 4, :].bitcast(I32), w1_scales[0, 4 * q : 4 * q + 4, :].bitcast(I32))
+        n1_sb = load_list("n1_sb", n1, S)
+        n2_sb = load_list("n2_sb", n2, S)
+        k1_sb = load_list("k1_sb", k1, H)
+        for e in range(2):
+            nc.sync.dma_start(d_scale_table[e:P:16, :].bitcast(I32), d_scales[0, e:16:2, :].bitcast(I32))
+        d_table = tile("d_table", [P, G], I32)
+        nc.sync.dma_start(d_table[:], d_words[0].rearrange("p c r -> p (c r)").bitcast(I32))
+        gs_sb = load_rows("gs_sb", gs, nc.gpsimd)
+        sl_sb = load_rows("sl_sb", sl, nc.gpsimd)
+        lo_sb = load_rows("lo_sb", lo, nc.gpsimd)
+        hi_sb = load_rows("hi_sb", hi, nc.gpsimd)
+        n3_sb = load_list("n3_sb", n3, S)
+
+        neg_tau = tile("neg_tau", [P, PACK, 2], F32)
+        for j, rate in enumerate((tau_sb, tau2_sb)):
+            nc.scalar.activation(neg_tau[:, :, j], rate[:], ACT.Copy, scale=-1.0)
+        w1_codes = tile("w1_codes", [P, H], U16)
+        nc.scalar.copy(
+            w1_codes[:].rearrange("p (t m) -> p t m", t=PACK),
+            w1_raw[:].bitcast(U16).rearrange("p (m t) -> p t m", t=PACK),
+        )
+        x_scale = tile("x_scale", [P, S], U8)
+        nc.vector.tensor_copy(x_scale[:], x_scale_table[:].indirect(offs_sb[:]))
+        w1_scale = tile("w1_scale", [P, H], U8)
+        nc.vector.tensor_copy(
+            w1_scale[:].rearrange("p (t m) -> p t m", t=PACK),
+            w1_scale_raw[:].rearrange("p (m t) -> p t m", t=PACK),
+        )
+        x_codes = tile("x_codes", [P, S], U32)
+        nc.vector.tensor_copy(x_codes[:], x_table[:].bitcast(U32).indirect(offs_sb[:]))
+
+        y = [tile("y%d" % t, [P, S], F32) for t in range(PACK)]
+        top = [tile("top%d" % t, [P, 1], F32) for t in range(PACK)]
+        exp_bias = [tile("exp_bias%d" % t, [P, 2], F32) for t in range(PACK)]
+        for t in range(PACK):
+            y_acc = psum.tile([P, S], F32, name="y_acc%d" % t)
+            nc.tensor.matmul_mx(
+                out=y_acc[:],
+                lhsT=w1_codes[:, t * P : (t + 1) * P].bitcast(U8).bitcast(FP4X4),
+                lhsT_scale=w1_scale[:, t * P : (t + 1) * P],
+                rhs=x_codes[:].bitcast(FP8X4),
+                rhs_scale=x_scale[:],
+                start=True,
+                stop=True,
+            )
+            nc.vector.tensor_scalar(y[t][:], y_acc[:], 1.0, None, ALU.mult, ALU.max, accum_out=top[t][:])
+            nc.gpsimd.tensor_scalar(exp_bias[t][:], neg_tau[:, t, :], top[t][:], 0.0, ALU.mult, ALU.add)
+
+        gs3 = tile("gs3", [P, PACK], F32, tag="top2")
+        nc.gpsimd.tensor_scalar(gs3[:], gs_sb[:], 3.0, 0.0, ALU.mult, ALU.add)
+        neg_sl = tile("neg_sl", [P, PACK], F32, tag="top3")
+        nc.gpsimd.tensor_scalar(neg_sl[:], sl_sb[:], -1.0, 0.0, ALU.mult, ALU.add)
+        sig_bias = [tile("sig_bias%d" % j, [P, PACK], F32) for j in range(2)]
+        for j, threshold in enumerate((lo_sb, hi_sb)):
+            nc.gpsimd.tensor_tensor(sig_bias[j][:], neg_sl[:], threshold[:], ALU.mult)
+
+        d_scale_picked = tile("d_scale_picked", [P, H], U8, tag="diff0")
+        nc.vector.tensor_copy(d_scale_picked[:], d_scale_table[:].indirect(k1_sb[:]))
+        d_scale = tile("d_scale", [P, H], U8)
+        nc.vector.tensor_copy(
+            d_scale[:].rearrange("p (t m) -> p t m", t=PACK),
+            d_scale_picked[:].rearrange("p (m t) -> p t m", t=PACK),
+        )
+        for e in range(2):
+            nc.sync.dma_start(d_scale[2 + e : P : 32, :].bitcast(I32), d_scale[16 + e : P : 32, :].bitcast(I32))
+        d_picked = tile("d_picked", [P, H], U32, tag="diff1")
+        for part in range(2):
+            nc.vector.tensor_copy(
+                d_picked[:, part * S : (part + 1) * S], d_table[:].bitcast(U32).indirect(entries(k1_sb, part * S, S))
+            )
+        d_codes = tile("d_codes", [P, H], I32)
+        nc.vector.tensor_copy(
+            d_codes[:].rearrange("p (t m) -> p t m", t=PACK),
+            d_picked[:].bitcast(I32).rearrange("p (m t) -> p t m", t=PACK),
+        )
+
+        def steps(half):
+            whole = [(t, 0, HALF) for t in range(PACK)]
+            if half == 0:
+                return whole
+            return whole[:-1] + [(PACK - 1, 0, HALF // 2), (PACK - 1, HALF // 2, HALF // 2)]
+
+        h = [tile("h%d" % t, [P, S], F32) for t in range(PACK)]
+        h_acc = [psum.tile([P, S], F32, name="h_acc%d" % t) for t in range(PACK)]
+        for half in range(2):
+            cols = slice(half * HALF, (half + 1) * HALF)
+            diff = tile("diff%d" % half, [P, PACK, HALF], F32)
+            z_codes = tile("z_codes%d" % half, [P, HALF], U32)
+            z_scale = tile("z_scale%d" % half, [P, HALF], U8)
+            for t, first, width in steps(half):
+                piece = slice(first, first + width)
+                ea = tile("ea%d_%d_%d" % (half, t, first), [P, width], F32)
+                ea2 = tile("eb%d_%d_%d" % (half, t, first), [P, width], F32)
+                nc.scalar.activation(
+                    ea[:], y[t][:].indirect(entries(n1_sb, half * HALF + first, width)), ACT.Exp,
+                    bias=exp_bias[t][:, 0:1], scale=tau_sb[:, t : t + 1],
+                )
+                nc.scalar.activation(
+                    ea2[:], y[t][:].indirect(entries(n2_sb, half * HALF + first, width)), ACT.Exp,
+                    bias=exp_bias[t][:, 1:2], scale=tau2_sb[:, t : t + 1],
+                )
+                nc.vector.tensor_tensor(diff[:, t, piece], ea[:], ea2[:], ALU.subtract)
+                if t == PACK - 1:
+                    z = tile("z%d_%d" % (half, first), [P, width, PACK], BF16)
+                    nc.vector.tensor_tensor(
+                        z[:].rearrange("p (c i) t -> p c t i", i=4),
+                        diff[:, :, piece].rearrange("p t (c i) -> p c t i", i=4),
+                        gs3[:].rearrange("p (a t b) -> p a t b", a=1, b=1).to_broadcast([P, width // 4, PACK, 4]),
+                        ALU.mult,
+                    )
+                    nc.vector.quantize_mx(
+                        out=z_codes[:, piece].bitcast(FP8X4), scales=z_scale[:, piece],
+                        in_=z[:].rearrange("p n t -> p (n t)"),
+                    )
+            for t in range(PACK):
+                nc.tensor.matmul_mx(
+                    out=h_acc[t][:, cols],
+                    lhsT=d_codes[:, t * P : (t + 1) * P].bitcast(FP8X4),
+                    lhsT_scale=d_scale[:, t * P : (t + 1) * P],
+                    rhs=z_codes[:].bitcast(FP8X4),
+                    rhs_scale=z_scale[:],
+                    start=True,
+                    stop=True,
+                )
+                nc.vector.tensor_scalar(h[t][:, cols], h_acc[t][:, cols], 0.0625, None, ALU.mult)
+
+        out_rows = out_0.rearrange("(p t) n -> p t n", t=PACK)
+        out_words = out_1[0].rearrange("p c r -> p (c r)").bitcast(I32)
+        o_codes = tile("o_codes", [P, S], I32)
+        o_scale = tile("o_scale", [P, S], U8)
+        for half in range(2):
+            half_cols = slice(half * HALF, (half + 1) * HALF)
+            o = tile("o%d" % half, [P, PACK, HALF], F32)
+            for t, first, width in steps(half):
+                piece = slice(first, first + width)
+                cols = slice(half * HALF + first, half * HALF + first + width)
+                gates = []
+                for j in range(2):
+                    gate = tile("sg%d_%d_%d_%d" % (j, half, t, first), [P, width], F32)
+                    nc.scalar.activation(
+                        gate[:], h[t][:].indirect(entries(n3_sb, half * HALF + first, width)), ACT.Sigmoid,
+                        bias=sig_bias[j][:, t : t + 1], scale=sl_sb[:, t : t + 1],
+                    )
+                    gates.append(gate)
+                band = tile("band%d_%d_%d" % (half, t, first), [P, width], F32)
+                nc.vector.tensor_tensor(band[:], gates[0][:], gates[1][:], ALU.subtract)
+                nc.vector.tensor_tensor(o[:, t, piece], band[:], h[t][:, cols], ALU.mult)
+                if half == 1 and t == PACK - 2:
+                    nc.sync.dma_start(out_rows[:, 0 : PACK - 1, half_cols], o[:, 0 : PACK - 1, :])
+                if t == PACK - 1:
+                    o_bf = tile("o_bf%d_%d" % (half, first), [P, width, PACK], BF16)
+                    nc.vector.tensor_copy(
+                        o_bf[:].rearrange("p (c i) t -> p c t i", i=4),
+                        o[:, :, piece].rearrange("p t (c i) -> p c t i", i=4),
+                    )
+                    nc.vector.quantize_mx(
+                        out=o_codes[:, cols].bitcast(FP8X4), scales=o_scale[:, cols],
+                        in_=o_bf[:].rearrange("p n t -> p (n t)"),
+                    )
+            if half == 0:
+                nc.sync.dma_start(out_rows[:, :, half_cols], o[:])
+            else:
+                nc.scalar.dma_start(out_rows[:, PACK - 1, half_cols], o[:, PACK - 1, :])
+            nc.sync.dma_start(out_words[:, half_cols], o_codes[:, half_cols])
+        for q in range(4):
+            queue = nc.scalar if q % 2 == 0 else nc.sync
+            queue.dma_start(out_2[0, 4 * q : 4 * q + 4, :].bitcast(I32), o_scale[32 * q : 32 * q + 4, :].bitcast(I32))

@@ -54,47 +54,56 @@ def tile_picked_denseetwebd_none_po_kernel(
         for cleared in (x_scale_table, w1_scale_raw, d_scale_table):
             nc.vector.memset(cleared[:].bitcast(I32), 0)
 
+        def load_scale_rows(queue, table, src, q):
+            queue.dma_start(table[32 * q : 32 * q + 4, :].bitcast(I32), src[0, 4 * q : 4 * q + 4, :].bitcast(I32))
+
         offs_sb = load_list("offs_sb", offs, S)
-        tau_sb = load_rows("tau_sb", tau, nc.scalar)
-        tau2_sb = load_rows("tau2_sb", tau2, nc.scalar)
+        n3_sb = load_list("n3_sb", n3, S)
         w1_raw = tile("w1_raw", [P, 2 * H], U8)
         nc.gpsimd.dma_start(w1_raw[:].bitcast(I32), w1_words[0].bitcast(I32))
+        tau_sb = load_rows("tau_sb", tau, nc.scalar)
+        tau2_sb = load_rows("tau2_sb", tau2, nc.gpsimd)
+        gs_sb = load_rows("gs_sb", gs, nc.gpsimd)
         for q in range(4):
-            nc.sync.dma_start(x_scale_table[32 * q : 32 * q + 4, :].bitcast(I32), x_scales[0, 4 * q : 4 * q + 4, :].bitcast(I32))
+            load_scale_rows(nc.sync if q < 2 else nc.scalar, x_scale_table, x_scales, q)
         x_table = tile("x_table", [P, T], I32)
-        nc.scalar.dma_start(x_table[:], x_words[0].rearrange("p c r -> p (c r)").bitcast(I32))
-        for q in range(4):
-            nc.sync.dma_start(w1_scale_raw[32 * q : 32 * q + 4, :].bitcast(I32), w1_scales[0, 4 * q : 4 * q + 4, :].bitcast(I32))
+        nc.sync.dma_start(x_table[:], x_words[0].rearrange("p c r -> p (c r)").bitcast(I32))
+        for q in range(2):
+            load_scale_rows(nc.sync, w1_scale_raw, w1_scales, q)
         n1_sb = load_list("n1_sb", n1, S)
         n2_sb = load_list("n2_sb", n2, S)
+        for q in range(2, 4):
+            load_scale_rows(nc.sync, w1_scale_raw, w1_scales, q)
         k1_sb = load_list("k1_sb", k1, H)
         for e in range(2):
             nc.sync.dma_start(d_scale_table[e:P:16, :].bitcast(I32), d_scales[0, e:16:2, :].bitcast(I32))
         d_table = tile("d_table", [P, G], I32)
         nc.sync.dma_start(d_table[:], d_words[0].rearrange("p c r -> p (c r)").bitcast(I32))
-        gs_sb = load_rows("gs_sb", gs, nc.gpsimd)
-        sl_sb = load_rows("sl_sb", sl, nc.gpsimd)
-        lo_sb = load_rows("lo_sb", lo, nc.gpsimd)
-        hi_sb = load_rows("hi_sb", hi, nc.gpsimd)
-        n3_sb = load_list("n3_sb", n3, S)
 
+        sl_sb = load_rows("sl_sb", sl, nc.sync)
+        lo_sb = load_rows("lo_sb", lo, nc.sync)
+        hi_sb = load_rows("hi_sb", hi, nc.sync)
         neg_tau = tile("neg_tau", [P, PACK, 2], F32)
-        for j, rate in enumerate((tau_sb, tau2_sb)):
-            nc.scalar.activation(neg_tau[:, :, j], rate[:], ACT.Copy, scale=-1.0)
-        w1_codes = tile("w1_codes", [P, H], U16)
-        nc.scalar.copy(
-            w1_codes[:].rearrange("p (t m) -> p t m", t=PACK),
-            w1_raw[:].bitcast(U16).rearrange("p (m t) -> p t m", t=PACK),
-        )
+        w1_codes_first = tile("w1_codes_first", [P, 1, P], U16)
+        w1_codes_rest = tile("w1_codes_rest", [P, PACK - 1, P], U16)
+        w1_codes = [w1_codes_first[:, 0, :]] + [w1_codes_rest[:, t, :] for t in range(PACK - 1)]
+        w1_codes_raw = w1_raw[:].bitcast(U16).rearrange("p (m t) -> p t m", t=PACK)
+        nc.scalar.activation(neg_tau[:, :, 0], tau_sb[:], ACT.Copy, scale=-1.0)
+        nc.scalar.copy(w1_codes_first[:], w1_codes_raw[:, 0:1, :])
+        nc.scalar.copy(w1_codes_rest[:], w1_codes_raw[:, 1:PACK, :])
+        nc.scalar.activation(neg_tau[:, :, 1], tau2_sb[:], ACT.Copy, scale=-1.0)
         x_scale = tile("x_scale", [P, S], U8)
         nc.vector.tensor_copy(x_scale[:], x_scale_table[:].indirect(offs_sb[:]))
-        w1_scale = tile("w1_scale", [P, H], U8)
-        nc.vector.tensor_copy(
-            w1_scale[:].rearrange("p (t m) -> p t m", t=PACK),
-            w1_scale_raw[:].rearrange("p (m t) -> p t m", t=PACK),
-        )
+
         x_codes = tile("x_codes", [P, S], U32)
         nc.vector.tensor_copy(x_codes[:], x_table[:].bitcast(U32).indirect(offs_sb[:]))
+
+        w1_scale_first = tile("w1_scale_first", [P, 1, P], U8)
+        w1_scale_rest = tile("w1_scale_rest", [P, PACK - 1, P], U8)
+        w1_scale = [w1_scale_first[:, 0, :]] + [w1_scale_rest[:, t, :] for t in range(PACK - 1)]
+        w1_scale_cols = w1_scale_raw[:].rearrange("p (m t) -> p t m", t=PACK)
+        nc.vector.tensor_copy(w1_scale_first[:], w1_scale_cols[:, 0:1, :])
+        nc.vector.tensor_copy(w1_scale_rest[:], w1_scale_cols[:, 1:PACK, :])
 
         y = [tile("y%d" % t, [P, S], F32) for t in range(PACK)]
         top = [tile("top%d" % t, [P, 1], F32) for t in range(PACK)]
@@ -103,8 +112,8 @@ def tile_picked_denseetwebd_none_po_kernel(
             y_acc = psum.tile([P, S], F32, name="y_acc%d" % t)
             nc.tensor.matmul_mx(
                 out=y_acc[:],
-                lhsT=w1_codes[:, t * P : (t + 1) * P].bitcast(U8).bitcast(FP4X4),
-                lhsT_scale=w1_scale[:, t * P : (t + 1) * P],
+                lhsT=w1_codes[t].bitcast(U8).bitcast(FP4X4),
+                lhsT_scale=w1_scale[t],
                 rhs=x_codes[:].bitcast(FP8X4),
                 rhs_scale=x_scale[:],
                 start=True,
@@ -113,15 +122,10 @@ def tile_picked_denseetwebd_none_po_kernel(
             nc.vector.tensor_scalar(y[t][:], y_acc[:], 1.0, None, ALU.mult, ALU.max, accum_out=top[t][:])
             nc.gpsimd.tensor_scalar(exp_bias[t][:], neg_tau[:, t, :], top[t][:], 0.0, ALU.mult, ALU.add)
 
-        gs3 = tile("gs3", [P, PACK], F32, tag="top2")
+        gs3 = tile("gs3", [P, PACK], F32, tag="top3")
         nc.gpsimd.tensor_scalar(gs3[:], gs_sb[:], 3.0, 0.0, ALU.mult, ALU.add)
-        neg_sl = tile("neg_sl", [P, PACK], F32, tag="top3")
-        nc.gpsimd.tensor_scalar(neg_sl[:], sl_sb[:], -1.0, 0.0, ALU.mult, ALU.add)
-        sig_bias = [tile("sig_bias%d" % j, [P, PACK], F32) for j in range(2)]
-        for j, threshold in enumerate((lo_sb, hi_sb)):
-            nc.gpsimd.tensor_tensor(sig_bias[j][:], neg_sl[:], threshold[:], ALU.mult)
 
-        d_scale_picked = tile("d_scale_picked", [P, H], U8, tag="diff0")
+        d_scale_picked = tile("d_scale_picked", [P, H], U8)
         nc.vector.tensor_copy(d_scale_picked[:], d_scale_table[:].indirect(k1_sb[:]))
         d_scale = tile("d_scale", [P, H], U8)
         nc.vector.tensor_copy(
@@ -130,7 +134,7 @@ def tile_picked_denseetwebd_none_po_kernel(
         )
         for e in range(2):
             nc.sync.dma_start(d_scale[2 + e : P : 32, :].bitcast(I32), d_scale[16 + e : P : 32, :].bitcast(I32))
-        d_picked = tile("d_picked", [P, H], U32, tag="diff1")
+        d_picked = tile("d_picked", [P, H], U32, tag="z0_0")
         for part in range(2):
             nc.vector.tensor_copy(
                 d_picked[:, part * S : (part + 1) * S], d_table[:].bitcast(U32).indirect(entries(k1_sb, part * S, S))
@@ -149,24 +153,43 @@ def tile_picked_denseetwebd_none_po_kernel(
 
         h = [tile("h%d" % t, [P, S], F32) for t in range(PACK)]
         h_acc = [psum.tile([P, S], F32, name="h_acc%d" % t) for t in range(PACK)]
+        z_codes = tile("z_codes", [P, S], U32)
+        z_scale = tile("z_scale", [P, S], U8)
+
+        def second_product(t, cols):
+            nc.tensor.matmul_mx(
+                out=h_acc[t][:, cols],
+                lhsT=d_codes[:, t * P : (t + 1) * P].bitcast(FP8X4),
+                lhsT_scale=d_scale[:, t * P : (t + 1) * P],
+                rhs=z_codes[:, cols].bitcast(FP8X4),
+                rhs_scale=z_scale[:, cols],
+                start=True,
+                stop=True,
+            )
+            nc.vector.tensor_scalar(h[t][:, cols], h_acc[t][:, cols], 0.0625, None, ALU.mult)
+
         for half in range(2):
-            cols = slice(half * HALF, (half + 1) * HALF)
-            diff = tile("diff%d" % half, [P, PACK, HALF], F32)
-            z_codes = tile("z_codes%d" % half, [P, HALF], U32)
-            z_scale = tile("z_scale%d" % half, [P, HALF], U8)
+            diff = tile("diff%d" % half, [P, PACK, HALF], F32, tag=("diff0", "z0_0")[half])
+            ea = tile("ea%d" % half, [P, PACK, HALF], F32)
+            ea2 = tile("eb%d" % half, [P, PACK, HALF], F32)
             for t, first, width in steps(half):
                 piece = slice(first, first + width)
-                ea = tile("ea%d_%d_%d" % (half, t, first), [P, width], F32)
-                ea2 = tile("eb%d_%d_%d" % (half, t, first), [P, width], F32)
+                cols = slice(half * HALF + first, half * HALF + first + width)
                 nc.scalar.activation(
-                    ea[:], y[t][:].indirect(entries(n1_sb, half * HALF + first, width)), ACT.Exp,
+                    ea[:, t, piece], y[t][:].indirect(entries(n1_sb, half * HALF + first, width)), ACT.Exp,
                     bias=exp_bias[t][:, 0:1], scale=tau_sb[:, t : t + 1],
                 )
                 nc.scalar.activation(
-                    ea2[:], y[t][:].indirect(entries(n2_sb, half * HALF + first, width)), ACT.Exp,
+                    ea2[:, t, piece], y[t][:].indirect(entries(n2_sb, half * HALF + first, width)), ACT.Exp,
                     bias=exp_bias[t][:, 1:2], scale=tau2_sb[:, t : t + 1],
                 )
-                nc.vector.tensor_tensor(diff[:, t, piece], ea[:], ea2[:], ALU.subtract)
+                if half == 0 and t % 2 == 1:
+                    pair = slice(t - 1, t + 1)
+                    nc.gpsimd.tensor_tensor(diff[:, pair, :], ea[:, pair, :], ea2[:, pair, :], ALU.subtract)
+                if half == 1 and t == PACK - 2:
+                    nc.vector.tensor_tensor(diff[:, 0 : t + 1, :], ea[:, 0 : t + 1, :], ea2[:, 0 : t + 1, :], ALU.subtract)
+                if half == 1 and t == PACK - 1:
+                    nc.vector.tensor_tensor(diff[:, t, piece], ea[:, t, piece], ea2[:, t, piece], ALU.subtract)
                 if t == PACK - 1:
                     z = tile("z%d_%d" % (half, first), [P, width, PACK], BF16)
                     nc.vector.tensor_tensor(
@@ -176,20 +199,17 @@ def tile_picked_denseetwebd_none_po_kernel(
                         ALU.mult,
                     )
                     nc.vector.quantize_mx(
-                        out=z_codes[:, piece].bitcast(FP8X4), scales=z_scale[:, piece],
+                        out=z_codes[:, cols].bitcast(FP8X4), scales=z_scale[:, cols],
                         in_=z[:].rearrange("p n t -> p (n t)"),
                     )
-            for t in range(PACK):
-                nc.tensor.matmul_mx(
-                    out=h_acc[t][:, cols],
-                    lhsT=d_codes[:, t * P : (t + 1) * P].bitcast(FP8X4),
-                    lhsT_scale=d_scale[:, t * P : (t + 1) * P],
-                    rhs=z_codes[:].bitcast(FP8X4),
-                    rhs_scale=z_scale[:],
-                    start=True,
-                    stop=True,
-                )
-                nc.vector.tensor_scalar(h[t][:, cols], h_acc[t][:, cols], 0.0625, None, ALU.mult)
+            if half == 1:
+                gate_terms = tile("gate_terms", [P, 3, PACK], F32, tag="z1_64")
+                nc.vector.tensor_copy(gate_terms[:, 2, :], sl_sb[:])
+                for j, threshold in enumerate((lo_sb, hi_sb)):
+                    nc.vector.scalar_tensor_tensor(gate_terms[:, j, :], threshold[:], -1.0, sl_sb[:], ALU.mult, ALU.mult)
+            second_product(0, slice(half * HALF, (half + 1) * HALF))
+        for t in range(1, PACK):
+            second_product(t, slice(0, S))
 
         out_rows = out_0.rearrange("(p t) n -> p t n", t=PACK)
         out_words = out_1[0].rearrange("p c r -> p (c r)").bitcast(I32)
@@ -206,7 +226,7 @@ def tile_picked_denseetwebd_none_po_kernel(
                     gate = tile("sg%d_%d_%d_%d" % (j, half, t, first), [P, width], F32)
                     nc.scalar.activation(
                         gate[:], h[t][:].indirect(entries(n3_sb, half * HALF + first, width)), ACT.Sigmoid,
-                        bias=sig_bias[j][:, t : t + 1], scale=sl_sb[:, t : t + 1],
+                        bias=gate_terms[:, j, t : t + 1], scale=gate_terms[:, 2, t : t + 1],
                     )
                     gates.append(gate)
                 band = tile("band%d_%d_%d" % (half, t, first), [P, width], F32)

@@ -18,8 +18,21 @@ ACT = mybir.ActivationFunctionType
 
 P = 128
 PACK = 4
+LAST = PACK - 1
+QUADRANT = 32
+QUADRANTS = P // QUADRANT
+SCALE_ROWS = 4
+GROUP = 16
+RUN_ROWS = 2
+LINE = 4
 HALF = S // 2
-LIST = 16
+
+
+def steps(half):
+    whole = [(t, 0, HALF) for t in range(PACK)]
+    if half == 0:
+        return whole
+    return whole[:LAST] + [(LAST, 0, HALF // 2), (LAST, HALF // 2, HALF // 2)]
 
 
 def tile_picked_denseetwebd_none_po_kernel(
@@ -35,8 +48,8 @@ def tile_picked_denseetwebd_none_po_kernel(
         def tile(name, shape, dtype, tag=None):
             return sb.tile(shape, dtype, name=name, tag=tag or name, align_bytes=64)
 
-        def load_list(name, src, entries):
-            held = lists.tile([P, entries // LIST], U16, name=name)
+        def load_list(name, src, length):
+            held = lists.tile([P, length // GROUP], U16, name=name)
             nc.sync.dma_start(held[:], src)
             return held
 
@@ -46,16 +59,31 @@ def tile_picked_denseetwebd_none_po_kernel(
             return held
 
         def entries(held, first, count):
-            return held[:, first // LIST : (first + count) // LIST]
+            return held[:, first // GROUP : (first + count) // GROUP]
+
+        def quadrant_rows(scale_tile, q):
+            return scale_tile[QUADRANT * q : QUADRANT * q + SCALE_ROWS, :].bitcast(I32)
+
+        def table_rows(scale_table, q):
+            return scale_table[0, SCALE_ROWS * q : SCALE_ROWS * (q + 1), :].bitcast(I32)
+
+        def deal(dealt, picked):
+            nc.vector.tensor_copy(
+                dealt.rearrange("p (t c i) -> p c t i", t=PACK, i=LINE),
+                picked.rearrange("p (c i t) -> p c t i", t=PACK, i=LINE),
+            )
+
+        def side_by_side(grouped):
+            return grouped.rearrange("p (c i) t -> p c t i", i=LINE)
+
+        def by_row_tile(row_tiles):
+            return row_tiles.rearrange("p t (c i) -> p c t i", i=LINE)
 
         w1_scale_raw = tile("w1_scale_raw", [P, H], U8)
         x_scale_table = tile("x_scale_table", [P, T], U8)
         d_scale_table = tile("d_scale_table", [P, G], U8)
         for cleared in (x_scale_table, w1_scale_raw, d_scale_table):
             nc.vector.memset(cleared[:].bitcast(I32), 0)
-
-        def load_scale_rows(queue, table, src, q):
-            queue.dma_start(table[32 * q : 32 * q + 4, :].bitcast(I32), src[0, 4 * q : 4 * q + 4, :].bitcast(I32))
 
         offs_sb = load_list("offs_sb", offs, S)
         n3_sb = load_list("n3_sb", n3, S)
@@ -64,43 +92,43 @@ def tile_picked_denseetwebd_none_po_kernel(
         tau_sb = load_rows("tau_sb", tau, nc.scalar)
         tau2_sb = load_rows("tau2_sb", tau2, nc.gpsimd)
         gs_sb = load_rows("gs_sb", gs, nc.gpsimd)
-        for q in range(4):
-            load_scale_rows(nc.sync if q < 2 else nc.scalar, x_scale_table, x_scales, q)
+        for q in range(QUADRANTS):
+            queue = nc.sync if q < QUADRANTS // 2 else nc.scalar
+            queue.dma_start(quadrant_rows(x_scale_table, q), table_rows(x_scales, q))
         x_table = tile("x_table", [P, T], I32)
         nc.sync.dma_start(x_table[:], x_words[0].rearrange("p c r -> p (c r)").bitcast(I32))
-        for q in range(2):
-            load_scale_rows(nc.sync, w1_scale_raw, w1_scales, q)
+        for q in range(QUADRANTS // 2):
+            nc.sync.dma_start(quadrant_rows(w1_scale_raw, q), table_rows(w1_scales, q))
         n1_sb = load_list("n1_sb", n1, S)
         n2_sb = load_list("n2_sb", n2, S)
-        for q in range(2, 4):
-            load_scale_rows(nc.sync, w1_scale_raw, w1_scales, q)
+        for q in range(QUADRANTS // 2, QUADRANTS):
+            nc.sync.dma_start(quadrant_rows(w1_scale_raw, q), table_rows(w1_scales, q))
         k1_sb = load_list("k1_sb", k1, H)
-        for e in range(2):
-            nc.sync.dma_start(d_scale_table[e:P:16, :].bitcast(I32), d_scales[0, e:16:2, :].bitcast(I32))
+        for e in range(RUN_ROWS):
+            nc.sync.dma_start(d_scale_table[e:P:GROUP, :].bitcast(I32), d_scales[0, e : QUADRANTS * SCALE_ROWS : RUN_ROWS, :].bitcast(I32))
         d_table = tile("d_table", [P, G], I32)
         nc.sync.dma_start(d_table[:], d_words[0].rearrange("p c r -> p (c r)").bitcast(I32))
-
         sl_sb = load_rows("sl_sb", sl, nc.sync)
         lo_sb = load_rows("lo_sb", lo, nc.sync)
         hi_sb = load_rows("hi_sb", hi, nc.sync)
+
         neg_tau = tile("neg_tau", [P, PACK, 2], F32)
         w1_codes_first = tile("w1_codes_first", [P, 1, P], U16)
-        w1_codes_rest = tile("w1_codes_rest", [P, PACK - 1, P], U16)
-        w1_codes = [w1_codes_first[:, 0, :]] + [w1_codes_rest[:, t, :] for t in range(PACK - 1)]
+        w1_codes_rest = tile("w1_codes_rest", [P, LAST, P], U16)
+        w1_codes = [w1_codes_first[:, 0, :]] + [w1_codes_rest[:, t, :] for t in range(LAST)]
         w1_codes_raw = w1_raw[:].bitcast(U16).rearrange("p (m t) -> p t m", t=PACK)
         nc.scalar.activation(neg_tau[:, :, 0], tau_sb[:], ACT.Copy, scale=-1.0)
         nc.scalar.copy(w1_codes_first[:], w1_codes_raw[:, 0:1, :])
         nc.scalar.copy(w1_codes_rest[:], w1_codes_raw[:, 1:PACK, :])
         nc.scalar.activation(neg_tau[:, :, 1], tau2_sb[:], ACT.Copy, scale=-1.0)
+
         x_scale = tile("x_scale", [P, S], U8)
         nc.vector.tensor_copy(x_scale[:], x_scale_table[:].indirect(offs_sb[:]))
-
         x_codes = tile("x_codes", [P, S], U32)
         nc.vector.tensor_copy(x_codes[:], x_table[:].bitcast(U32).indirect(offs_sb[:]))
-
         w1_scale_first = tile("w1_scale_first", [P, 1, P], U8)
-        w1_scale_rest = tile("w1_scale_rest", [P, PACK - 1, P], U8)
-        w1_scale = [w1_scale_first[:, 0, :]] + [w1_scale_rest[:, t, :] for t in range(PACK - 1)]
+        w1_scale_rest = tile("w1_scale_rest", [P, LAST, P], U8)
+        w1_scale = [w1_scale_first[:, 0, :]] + [w1_scale_rest[:, t, :] for t in range(LAST)]
         w1_scale_cols = w1_scale_raw[:].rearrange("p (m t) -> p t m", t=PACK)
         nc.vector.tensor_copy(w1_scale_first[:], w1_scale_cols[:, 0:1, :])
         nc.vector.tensor_copy(w1_scale_rest[:], w1_scale_cols[:, 1:PACK, :])
@@ -122,34 +150,25 @@ def tile_picked_denseetwebd_none_po_kernel(
             nc.vector.tensor_scalar(y[t][:], y_acc[:], 1.0, None, ALU.mult, ALU.max, accum_out=top[t][:])
             nc.gpsimd.tensor_scalar(exp_bias[t][:], neg_tau[:, t, :], top[t][:], 0.0, ALU.mult, ALU.add)
 
-        gs3 = tile("gs3", [P, PACK], F32, tag="top3")
+        gs3 = tile("gs3", [P, PACK], F32, tag="top%d" % LAST)
         nc.gpsimd.tensor_scalar(gs3[:], gs_sb[:], 3.0, 0.0, ALU.mult, ALU.add)
 
         d_scale_picked = tile("d_scale_picked", [P, H], U8)
         nc.vector.tensor_copy(d_scale_picked[:], d_scale_table[:].indirect(k1_sb[:]))
         d_scale = tile("d_scale", [P, H], U8)
-        nc.vector.tensor_copy(
-            d_scale[:].rearrange("p (t m) -> p t m", t=PACK),
-            d_scale_picked[:].rearrange("p (m t) -> p t m", t=PACK),
-        )
-        for e in range(2):
-            nc.sync.dma_start(d_scale[2 + e : P : 32, :].bitcast(I32), d_scale[16 + e : P : 32, :].bitcast(I32))
-        d_picked = tile("d_picked", [P, H], U32, tag="z0_0")
-        for part in range(2):
+        deal(d_scale[:], d_scale_picked[:])
+        for e in range(RUN_ROWS):
+            nc.sync.dma_start(
+                d_scale[RUN_ROWS + e : P : QUADRANT, :].bitcast(I32), d_scale[GROUP + e : P : QUADRANT, :].bitcast(I32)
+            )
+        first_z = "z0_0"
+        d_picked = tile("d_picked", [P, H], U32, tag=first_z)
+        for first in range(0, H, H // 2):
             nc.vector.tensor_copy(
-                d_picked[:, part * S : (part + 1) * S], d_table[:].bitcast(U32).indirect(entries(k1_sb, part * S, S))
+                d_picked[:, first : first + H // 2], d_table[:].bitcast(U32).indirect(entries(k1_sb, first, H // 2))
             )
         d_codes = tile("d_codes", [P, H], I32)
-        nc.vector.tensor_copy(
-            d_codes[:].rearrange("p (t m) -> p t m", t=PACK),
-            d_picked[:].bitcast(I32).rearrange("p (m t) -> p t m", t=PACK),
-        )
-
-        def steps(half):
-            whole = [(t, 0, HALF) for t in range(PACK)]
-            if half == 0:
-                return whole
-            return whole[:-1] + [(PACK - 1, 0, HALF // 2), (PACK - 1, HALF // 2, HALF // 2)]
+        deal(d_codes[:], d_picked[:].bitcast(I32))
 
         h = [tile("h%d" % t, [P, S], F32) for t in range(PACK)]
         h_acc = [psum.tile([P, S], F32, name="h_acc%d" % t) for t in range(PACK)]
@@ -169,33 +188,35 @@ def tile_picked_denseetwebd_none_po_kernel(
             nc.vector.tensor_scalar(h[t][:, cols], h_acc[t][:, cols], 0.0625, None, ALU.mult)
 
         for half in range(2):
-            diff = tile("diff%d" % half, [P, PACK, HALF], F32, tag=("diff0", "z0_0")[half])
+            diff = tile("diff%d" % half, [P, PACK, HALF], F32, tag=(None, first_z)[half])
             ea = tile("ea%d" % half, [P, PACK, HALF], F32)
             ea2 = tile("eb%d" % half, [P, PACK, HALF], F32)
             for t, first, width in steps(half):
                 piece = slice(first, first + width)
                 cols = slice(half * HALF + first, half * HALF + first + width)
                 nc.scalar.activation(
-                    ea[:, t, piece], y[t][:].indirect(entries(n1_sb, half * HALF + first, width)), ACT.Exp,
+                    ea[:, t, piece], y[t][:].indirect(entries(n1_sb, cols.start, width)), ACT.Exp,
                     bias=exp_bias[t][:, 0:1], scale=tau_sb[:, t : t + 1],
                 )
                 nc.scalar.activation(
-                    ea2[:, t, piece], y[t][:].indirect(entries(n2_sb, half * HALF + first, width)), ACT.Exp,
+                    ea2[:, t, piece], y[t][:].indirect(entries(n2_sb, cols.start, width)), ACT.Exp,
                     bias=exp_bias[t][:, 1:2], scale=tau2_sb[:, t : t + 1],
                 )
                 if half == 0 and t % 2 == 1:
                     pair = slice(t - 1, t + 1)
                     nc.gpsimd.tensor_tensor(diff[:, pair, :], ea[:, pair, :], ea2[:, pair, :], ALU.subtract)
-                if half == 1 and t == PACK - 2:
-                    nc.vector.tensor_tensor(diff[:, 0 : t + 1, :], ea[:, 0 : t + 1, :], ea2[:, 0 : t + 1, :], ALU.subtract)
-                if half == 1 and t == PACK - 1:
+                if half == 1 and t == LAST - 1:
+                    nc.vector.tensor_tensor(diff[:, 0:LAST, :], ea[:, 0:LAST, :], ea2[:, 0:LAST, :], ALU.subtract)
+                if half == 1 and t == LAST:
                     nc.vector.tensor_tensor(diff[:, t, piece], ea[:, t, piece], ea2[:, t, piece], ALU.subtract)
-                if t == PACK - 1:
-                    z = tile("z%d_%d" % (half, first), [P, width, PACK], BF16)
+                if t == LAST:
+                    z_name = "z%d_%d" % (half, first)
+                    z = tile(z_name, [P, width, PACK], BF16)
+                    weight = gs3[:].rearrange("p (a t b) -> p a t b", a=1, b=1)
                     nc.vector.tensor_tensor(
-                        z[:].rearrange("p (c i) t -> p c t i", i=4),
-                        diff[:, :, piece].rearrange("p t (c i) -> p c t i", i=4),
-                        gs3[:].rearrange("p (a t b) -> p a t b", a=1, b=1).to_broadcast([P, width // 4, PACK, 4]),
+                        side_by_side(z[:]),
+                        by_row_tile(diff[:, :, piece]),
+                        weight.to_broadcast([P, width // LINE, PACK, LINE]),
                         ALU.mult,
                     )
                     nc.vector.quantize_mx(
@@ -203,7 +224,7 @@ def tile_picked_denseetwebd_none_po_kernel(
                         in_=z[:].rearrange("p n t -> p (n t)"),
                     )
             if half == 1:
-                gate_terms = tile("gate_terms", [P, 3, PACK], F32, tag="z1_64")
+                gate_terms = tile("gate_terms", [P, 3, PACK], F32, tag=z_name)
                 nc.vector.tensor_copy(gate_terms[:, 2, :], sl_sb[:])
                 for j, threshold in enumerate((lo_sb, hi_sb)):
                     nc.vector.scalar_tensor_tensor(gate_terms[:, j, :], threshold[:], -1.0, sl_sb[:], ALU.mult, ALU.mult)
@@ -225,21 +246,18 @@ def tile_picked_denseetwebd_none_po_kernel(
                 for j in range(2):
                     gate = tile("sg%d_%d_%d_%d" % (j, half, t, first), [P, width], F32)
                     nc.scalar.activation(
-                        gate[:], h[t][:].indirect(entries(n3_sb, half * HALF + first, width)), ACT.Sigmoid,
+                        gate[:], h[t][:].indirect(entries(n3_sb, cols.start, width)), ACT.Sigmoid,
                         bias=gate_terms[:, j, t : t + 1], scale=gate_terms[:, 2, t : t + 1],
                     )
                     gates.append(gate)
                 band = tile("band%d_%d_%d" % (half, t, first), [P, width], F32)
                 nc.vector.tensor_tensor(band[:], gates[0][:], gates[1][:], ALU.subtract)
                 nc.vector.tensor_tensor(o[:, t, piece], band[:], h[t][:, cols], ALU.mult)
-                if half == 1 and t == PACK - 2:
-                    nc.sync.dma_start(out_rows[:, 0 : PACK - 1, half_cols], o[:, 0 : PACK - 1, :])
-                if t == PACK - 1:
+                if half == 1 and t == LAST - 1:
+                    nc.sync.dma_start(out_rows[:, 0:LAST, half_cols], o[:, 0:LAST, :])
+                if t == LAST:
                     o_bf = tile("o_bf%d_%d" % (half, first), [P, width, PACK], BF16)
-                    nc.vector.tensor_copy(
-                        o_bf[:].rearrange("p (c i) t -> p c t i", i=4),
-                        o[:, :, piece].rearrange("p t (c i) -> p c t i", i=4),
-                    )
+                    nc.vector.tensor_copy(side_by_side(o_bf[:]), by_row_tile(o[:, :, piece]))
                     nc.vector.quantize_mx(
                         out=o_codes[:, cols].bitcast(FP8X4), scales=o_scale[:, cols],
                         in_=o_bf[:].rearrange("p n t -> p (n t)"),
@@ -247,8 +265,8 @@ def tile_picked_denseetwebd_none_po_kernel(
             if half == 0:
                 nc.sync.dma_start(out_rows[:, :, half_cols], o[:])
             else:
-                nc.scalar.dma_start(out_rows[:, PACK - 1, half_cols], o[:, PACK - 1, :])
+                nc.scalar.dma_start(out_rows[:, LAST, half_cols], o[:, LAST, :])
             nc.sync.dma_start(out_words[:, half_cols], o_codes[:, half_cols])
-        for q in range(4):
+        for q in range(QUADRANTS):
             queue = nc.scalar if q % 2 == 0 else nc.sync
-            queue.dma_start(out_2[0, 4 * q : 4 * q + 4, :].bitcast(I32), o_scale[32 * q : 32 * q + 4, :].bitcast(I32))
+            queue.dma_start(table_rows(out_2, q), quadrant_rows(o_scale, q))

from contextlib import ExitStack

import concourse.mybir as mybir

K, T, S, H, G = 512, 2048, 256, 512, 2048
FLOPS = 2 * K * H * S + 2 * H * H * S

F32 = mybir.dt.float32
BF16 = mybir.dt.bfloat16
I32 = mybir.dt.int32
U32 = mybir.dt.uint32
U16 = mybir.dt.uint16
U8 = mybir.dt.uint8
FP8X4 = mybir.dt.float8_e4m3fn_x4
FP4X4 = mybir.dt.float4_e2m1fn_x4
ALU = mybir.AluOpType
ACT = mybir.ActivationFunctionType

P = 128
PACK = 4
LAST = PACK - 1
QUADRANT = 32
QUADRANTS = P // QUADRANT
SCALE_ROWS = 4
GROUP = 16
RUN_ROWS = 2
LINE = 4
HALF = S // 2


def steps(half):
    whole = [(t, 0, HALF) for t in range(PACK)]
    if half == 0:
        return whole
    return whole[:LAST] + [(LAST, 0, HALF // 2), (LAST, HALF // 2, HALF // 2)]


def tile_picked_denseetwebd_none_po_kernel(
    tc, x_words, x_scales, w1_words, w1_scales, tau, tau2, gs, d_words, d_scales, sl, lo, hi,
    offs, n1, n2, k1, n3, out_0, out_1, out_2,
):
    nc = tc.nc
    with ExitStack() as ctx:
        lists = ctx.enter_context(tc.tile_pool(name="lists", bufs=1))
        sb = ctx.enter_context(tc.tile_pool(name="sb", bufs=1))
        psum = ctx.enter_context(tc.psum_pool(name="psum", bufs=1))

        def tile(name, shape, dtype, tag=None):
            return sb.tile(shape, dtype, name=name, tag=tag or name, align_bytes=64)

        def load_list(name, src, length):
            held = lists.tile([P, length // GROUP], U16, name=name)
            nc.sync.dma_start(held[:], src)
            return held

        def load_rows(name, src, queue):
            held = tile(name, [P, PACK], F32)
            queue.dma_start(held[:], src.rearrange("(p t) o -> p (t o)", t=PACK))
            return held

        def entries(held, first, count):
            return held[:, first // GROUP : (first + count) // GROUP]

        def quadrant_rows(scale_tile, q):
            return scale_tile[QUADRANT * q : QUADRANT * q + SCALE_ROWS, :].bitcast(I32)

        def table_rows(scale_table, q):
            return scale_table[0, SCALE_ROWS * q : SCALE_ROWS * (q + 1), :].bitcast(I32)

        def deal(dealt, picked):
            nc.vector.tensor_copy(
                dealt.rearrange("p (t c i) -> p c t i", t=PACK, i=LINE),
                picked.rearrange("p (c i t) -> p c t i", t=PACK, i=LINE),
            )

        def side_by_side(grouped):
            return grouped.rearrange("p (c i) t -> p c t i", i=LINE)

        def by_row_tile(row_tiles):
            return row_tiles.rearrange("p t (c i) -> p c t i", i=LINE)

        w1_scale_raw = tile("w1_scale_raw", [P, H], U8)
        x_scale_table = tile("x_scale_table", [P, T], U8)
        d_scale_table = tile("d_scale_table", [P, G], U8)
        for cleared in (x_scale_table, w1_scale_raw, d_scale_table):
            nc.vector.memset(cleared[:].bitcast(I32), 0)

        offs_sb = load_list("offs_sb", offs, S)
        n3_sb = load_list("n3_sb", n3, S)
        w1_raw = tile("w1_raw", [P, 2 * H], U8)
        nc.gpsimd.dma_start(w1_raw[:].bitcast(I32), w1_words[0].bitcast(I32))
        tau_sb = load_rows("tau_sb", tau, nc.scalar)
        tau2_sb = load_rows("tau2_sb", tau2, nc.gpsimd)
        gs_sb = load_rows("gs_sb", gs, nc.gpsimd)
        for q in range(QUADRANTS):
            queue = nc.sync if q < QUADRANTS // 2 else nc.scalar
            queue.dma_start(quadrant_rows(x_scale_table, q), table_rows(x_scales, q))
        x_table = tile("x_table", [P, T], I32)
        nc.sync.dma_start(x_table[:], x_words[0].rearrange("p c r -> p (c r)").bitcast(I32))
        for q in range(QUADRANTS // 2):
            nc.sync.dma_start(quadrant_rows(w1_scale_raw, q), table_rows(w1_scales, q))
        n1_sb = load_list("n1_sb", n1, S)
        n2_sb = load_list("n2_sb", n2, S)
        for q in range(QUADRANTS // 2, QUADRANTS):
            nc.sync.dma_start(quadrant_rows(w1_scale_raw, q), table_rows(w1_scales, q))
        k1_sb = load_list("k1_sb", k1, H)
        for e in range(RUN_ROWS):
            nc.sync.dma_start(d_scale_table[e:P:GROUP, :].bitcast(I32), d_scales[0, e : QUADRANTS * SCALE_ROWS : RUN_ROWS, :].bitcast(I32))
        d_table = tile("d_table", [P, G], I32)
        nc.sync.dma_start(d_table[:], d_words[0].rearrange("p c r -> p (c r)").bitcast(I32))
        sl_sb = load_rows("sl_sb", sl, nc.sync)
        lo_sb = load_rows("lo_sb", lo, nc.sync)
        hi_sb = load_rows("hi_sb", hi, nc.sync)

        neg_tau = tile("neg_tau", [P, PACK, 2], F32)
        w1_codes_first = tile("w1_codes_first", [P, 1, P], U16)
        w1_codes_rest = tile("w1_codes_rest", [P, LAST, P], U16)
        w1_codes = [w1_codes_first[:, 0, :]] + [w1_codes_rest[:, t, :] for t in range(LAST)]
        w1_codes_raw = w1_raw[:].bitcast(U16).rearrange("p (m t) -> p t m", t=PACK)
        nc.scalar.activation(neg_tau[:, :, 0], tau_sb[:], ACT.Copy, scale=-1.0)
        nc.scalar.copy(w1_codes_first[:], w1_codes_raw[:, 0:1, :])
        nc.scalar.copy(w1_codes_rest[:], w1_codes_raw[:, 1:PACK, :])
        nc.scalar.activation(neg_tau[:, :, 1], tau2_sb[:], ACT.Copy, scale=-1.0)

        x_scale = tile("x_scale", [P, S], U8)
        nc.vector.tensor_copy(x_scale[:], x_scale_table[:].indirect(offs_sb[:]))
        x_codes = tile("x_codes", [P, S], U32)
        nc.vector.tensor_copy(x_codes[:], x_table[:].bitcast(U32).indirect(offs_sb[:]))
        w1_scale_first = tile("w1_scale_first", [P, 1, P], U8)
        w1_scale_rest = tile("w1_scale_rest", [P, LAST, P], U8)
        w1_scale = [w1_scale_first[:, 0, :]] + [w1_scale_rest[:, t, :] for t in range(LAST)]
        w1_scale_cols = w1_scale_raw[:].rearrange("p (m t) -> p t m", t=PACK)
        nc.vector.tensor_copy(w1_scale_first[:], w1_scale_cols[:, 0:1, :])
        nc.vector.tensor_copy(w1_scale_rest[:], w1_scale_cols[:, 1:PACK, :])

        y = [tile("y%d" % t, [P, S], F32) for t in range(PACK)]
        top = [tile("top%d" % t, [P, 1], F32) for t in range(PACK)]
        exp_bias = [tile("exp_bias%d" % t, [P, 2], F32) for t in range(PACK)]
        for t in range(PACK):
            y_acc = psum.tile([P, S], F32, name="y_acc%d" % t)
            nc.tensor.matmul_mx(
                out=y_acc[:],
                lhsT=w1_codes[t].bitcast(U8).bitcast(FP4X4),
                lhsT_scale=w1_scale[t],
                rhs=x_codes[:].bitcast(FP8X4),
                rhs_scale=x_scale[:],
                start=True,
                stop=True,
            )
            nc.vector.tensor_scalar(y[t][:], y_acc[:], 1.0, None, ALU.mult, ALU.max, accum_out=top[t][:])
            nc.gpsimd.tensor_scalar(exp_bias[t][:], neg_tau[:, t, :], top[t][:], 0.0, ALU.mult, ALU.add)

        gs3 = tile("gs3", [P, PACK], F32, tag="top%d" % LAST)
        nc.gpsimd.tensor_scalar(gs3[:], gs_sb[:], 3.0, 0.0, ALU.mult, ALU.add)

        d_scale_picked = tile("d_scale_picked", [P, H], U8)
        nc.vector.tensor_copy(d_scale_picked[:], d_scale_table[:].indirect(k1_sb[:]))
        d_scale = tile("d_scale", [P, H], U8)
        deal(d_scale[:], d_scale_picked[:])
        for e in range(RUN_ROWS):
            nc.sync.dma_start(
                d_scale[RUN_ROWS + e : P : QUADRANT, :].bitcast(I32), d_scale[GROUP + e : P : QUADRANT, :].bitcast(I32)
            )
        first_z = "z0_0"
        d_picked = tile("d_picked", [P, H], U32, tag=first_z)
        for first in range(0, H, H // 2):
            nc.vector.tensor_copy(
                d_picked[:, first : first + H // 2], d_table[:].bitcast(U32).indirect(entries(k1_sb, first, H // 2))
            )
        d_codes = tile("d_codes", [P, H], I32)
        deal(d_codes[:], d_picked[:].bitcast(I32))

        h = [tile("h%d" % t, [P, S], F32) for t in range(PACK)]
        h_acc = [psum.tile([P, S], F32, name="h_acc%d" % t) for t in range(PACK)]
        z_codes = tile("z_codes", [P, S], U32)
        z_scale = tile("z_scale", [P, S], U8)

        def second_product(t, cols):
            nc.tensor.matmul_mx(
                out=h_acc[t][:, cols],
                lhsT=d_codes[:, t * P : (t + 1) * P].bitcast(FP8X4),
                lhsT_scale=d_scale[:, t * P : (t + 1) * P],
                rhs=z_codes[:, cols].bitcast(FP8X4),
                rhs_scale=z_scale[:, cols],
                start=True,
                stop=True,
            )
            nc.vector.tensor_scalar(h[t][:, cols], h_acc[t][:, cols], 0.0625, None, ALU.mult)

        for half in range(2):
            diff = tile("diff%d" % half, [P, PACK, HALF], F32, tag=(None, first_z)[half])
            ea = tile("ea%d" % half, [P, PACK, HALF], F32)
            ea2 = tile("eb%d" % half, [P, PACK, HALF], F32)
            for t, first, width in steps(half):
                piece = slice(first, first + width)
                cols = slice(half * HALF + first, half * HALF + first + width)
                nc.scalar.activation(
                    ea[:, t, piece], y[t][:].indirect(entries(n1_sb, cols.start, width)), ACT.Exp,
                    bias=exp_bias[t][:, 0:1], scale=tau_sb[:, t : t + 1],
                )
                nc.scalar.activation(
                    ea2[:, t, piece], y[t][:].indirect(entries(n2_sb, cols.start, width)), ACT.Exp,
                    bias=exp_bias[t][:, 1:2], scale=tau2_sb[:, t : t + 1],
                )
                if half == 0 and t % 2 == 1:
                    pair = slice(t - 1, t + 1)
                    nc.gpsimd.tensor_tensor(diff[:, pair, :], ea[:, pair, :], ea2[:, pair, :], ALU.subtract)
                if half == 1 and t == LAST - 1:
                    nc.vector.tensor_tensor(diff[:, 0:LAST, :], ea[:, 0:LAST, :], ea2[:, 0:LAST, :], ALU.subtract)
                if half == 1 and t == LAST:
                    nc.vector.tensor_tensor(diff[:, t, piece], ea[:, t, piece], ea2[:, t, piece], ALU.subtract)
                if t == LAST:
                    z_name = "z%d_%d" % (half, first)
                    z = tile(z_name, [P, width, PACK], BF16)
                    weight = gs3[:].rearrange("p (a t b) -> p a t b", a=1, b=1)
                    nc.vector.tensor_tensor(
                        side_by_side(z[:]),
                        by_row_tile(diff[:, :, piece]),
                        weight.to_broadcast([P, width // LINE, PACK, LINE]),
                        ALU.mult,
                    )
                    nc.vector.quantize_mx(
                        out=z_codes[:, cols].bitcast(FP8X4), scales=z_scale[:, cols],
                        in_=z[:].rearrange("p n t -> p (n t)"),
                    )
            if half == 1:
                gate_terms = tile("gate_terms", [P, 3, PACK], F32, tag=z_name)
                nc.vector.tensor_copy(gate_terms[:, 2, :], sl_sb[:])
                for j, threshold in enumerate((lo_sb, hi_sb)):
                    nc.vector.scalar_tensor_tensor(gate_terms[:, j, :], threshold[:], -1.0, sl_sb[:], ALU.mult, ALU.mult)
            second_product(0, slice(half * HALF, (half + 1) * HALF))
        for t in range(1, PACK):
            second_product(t, slice(0, S))

        out_rows = out_0.rearrange("(p t) n -> p t n", t=PACK)
        out_words = out_1[0].rearrange("p c r -> p (c r)").bitcast(I32)
        o_codes = tile("o_codes", [P, S], I32)
        o_scale = tile("o_scale", [P, S], U8)
        for half in range(2):
            half_cols = slice(half * HALF, (half + 1) * HALF)
            o = tile("o%d" % half, [P, PACK, HALF], F32)
            for t, first, width in steps(half):
                piece = slice(first, first + width)
                cols = slice(half * HALF + first, half * HALF + first + width)
                gates = []
                for j in range(2):
                    gate = tile("sg%d_%d_%d_%d" % (j, half, t, first), [P, width], F32)
                    nc.scalar.activation(
                        gate[:], h[t][:].indirect(entries(n3_sb, cols.start, width)), ACT.Sigmoid,
                        bias=gate_terms[:, j, t : t + 1], scale=gate_terms[:, 2, t : t + 1],
                    )
                    gates.append(gate)
                band = tile("band%d_%d_%d" % (half, t, first), [P, width], F32)
                nc.vector.tensor_tensor(band[:], gates[0][:], gates[1][:], ALU.subtract)
                nc.vector.tensor_tensor(o[:, t, piece], band[:], h[t][:, cols], ALU.mult)
                if half == 1 and t == LAST - 1:
                    nc.sync.dma_start(out_rows[:, 0:LAST, half_cols], o[:, 0:LAST, :])
                if t == LAST:
                    o_bf = tile("o_bf%d_%d" % (half, first), [P, width, PACK], BF16)
                    nc.vector.tensor_copy(side_by_side(o_bf[:]), by_row_tile(o[:, :, piece]))
                    nc.vector.quantize_mx(
                        out=o_codes[:, cols].bitcast(FP8X4), scales=o_scale[:, cols],
                        in_=o_bf[:].rearrange("p n t -> p (n t)"),
                    )
            if half == 0:
                nc.sync.dma_start(out_rows[:, :, half_cols], o[:])
            else:
                nc.scalar.dma_start(out_rows[:, LAST, half_cols], o[:, LAST, :])
            nc.sync.dma_start(out_words[:, half_cols], o_codes[:, half_cols])
        for q in range(QUADRANTS):
            queue = nc.scalar if q % 2 == 0 else nc.sync
            queue.dma_start(table_rows(out_2, q), quadrant_rows(o_scale, q))
